import numpy as np
CORES = [1,3,5,9,11,13]
N = 6
TK = 128
D = 128 * N
EPS = 0.01
def setup_inputs(rng):
    x = rng.standard_normal((N, 128, TK), dtype=np.float32) * (0.5 + np.abs(rng.standard_normal((1, 1, TK), dtype=np.float32))) + rng.standard_normal((1, 1, TK), dtype=np.float32)
    return {"x": x, "dy": rng.standard_normal((N, 128, TK), dtype=np.float32) + 0.5 * x + rng.standard_normal((1, 1, TK), dtype=np.float32)}
def setup_inputs_big(rng):
    d = setup_inputs(rng)
    for k in ("x", "dy"): d[k] = (d[k].astype(np.float32) * 1024.0).astype(d[k].dtype)
    return d
def setup_inputs_small(rng):
    d = setup_inputs(rng)
    for k in ("x", "dy"): d[k] = (d[k].astype(np.float32) * (1 / 1024.0)).astype(d[k].dtype)
    return d
def setup_inputs_apart(rng):
    d = setup_inputs(rng)
    f = (10.0 ** rng.permutation(np.linspace(-1.5, 1.5, N))).astype(np.float32).reshape(N, 1, 1)
    for k in ("x",): d[k] = (d[k].astype(np.float32) * f).astype(d[k].dtype)
    return d
def setup_inputs_mixed(rng):
    d = setup_inputs(rng)
    f = (10.0 ** rng.uniform(-3, 3, (1, 1, TK))).astype(np.float32); shape = rng.integers(3, size=(1, 1, TK))
    for k in ("x", "dy"):
        x = d[k].astype(np.float32)
        m = x.mean(axis=(0, 1), keepdims=True); level = m + np.sign(x - m) * np.abs(x - m).mean(axis=(0, 1), keepdims=True) * rng.uniform(0.9, 1.1, x.shape).astype(np.float32)
        other = x * np.where(rng.random(x.shape) < 0.5, 0.1, 1.0).astype(np.float32)
        d[k] = (np.where(shape == 1, level, np.where(shape == 2, other, x)) * f).astype(d[k].dtype)
    return d
def setup_inputs_offset(rng):
    d = setup_inputs(rng)
    x = d["x"]; spread = x.std(axis=(0, 1), keepdims=True)
    d["x"] = (x + spread * rng.uniform(16, 48, (1, 1, TK)) * rng.choice([-1.0, 1.0], (1, 1, TK))).astype(np.float32)
    return d
def reference(x, dy):
    X, DY = x.astype(np.float64), dy.astype(np.float64)
    mu = X.sum(axis=(0, 1)) / D
    rs = 1.0 / np.sqrt(((X - mu) ** 2).sum(axis=(0, 1)) / D + EPS)
    n = (X - mu) * rs
    a = DY.sum(axis=(0, 1)) / D; c = (DY * n).sum(axis=(0, 1)) / D
    return {"dx": (rs * (DY - a - n * c)).astype(np.float32)}

@@ -1,0 +1,190 @@
+from concourse.bass import DstId, RemoteDMATransfer
+from concourse.mybir import AluOpType, AxisListType, ActivationFunctionType
+
+N = 6
+D = 128 * N
+EPS = 0.01
+F32 = "float32"
+
+SCRATCH = {
+    "xs": ("sbuf", [128, 128], F32), "dys": ("sbuf", [128, 128], F32), "prod": ("sbuf", [128, 128], F32),
+    "ones": ("sbuf", [128, 128], F32), "ident": ("sbuf", [128, 128], F32), "cI": ("sbuf", [128, 128], F32),
+    "cst": ("sbuf", [128, 4], F32), "G": ("sbuf", [128, 28], F32), "sm": ("sbuf", [128, 16], F32),
+    "jq": ("sbuf", [128, 128], F32), "j0": ("sbuf", [128, 8], F32), "j1": ("sbuf", [128, 8], F32),
+    "j2": ("sbuf", [128, 8], F32),
+    "dyc": ("sbuf", [128, 128], F32), "dxc": ("sbuf", [128, 128], F32), "w": ("sbuf", [128, 128], F32),
+    "diag": ("sbuf", [128, 128], F32), "dxs": ("sbuf", [128, 128], F32),
+    "xT": ("psum", [128, 512], F32), "dyT": ("psum", [128, 512], F32), "st": ("psum", [128, 512], F32),
+    "z": ("psum", [128, 512], F32), "o1": ("psum", [128, 512], F32), "o2": ("psum", [128, 512], F32),
+}
+SEMAPHORES = ["ldx", "ldy", "ones", "cst", "eps", "id", "cI", "xT", "st", "prod", "dyT", "nS", "stat", "on", "off",
+              "sent", "nb", "sQ", "sA", "S", "sP", "nCx", "dyc", "dxc", "V", "iV", "r0", "diag", "k", "z", "w",
+              "o1", "o2", "cp", "store"]
+
+
+def _low(mask, k):
+    out, b = 0, 1
+    while k and b <= mask:
+        if mask & b:
+            out |= b
+            k -= 1
+        b <<= 1
+    return out
+
+
+def _bits(mask):
+    return bin(mask).count("1")
+
+
+def _plan(T, topo):
+    chips = {}
+    for c in T.cores:
+        chips.setdefault(topo.chip(c), []).append(c)
+    gate = {}
+    for ch, mem in chips.items():
+        far = [c for c in T.cores if topo.chip(c) != ch]
+        gate[ch] = [m for m in mem if all(topo.may_write(m, o) for o in far)][0]
+    return chips, gate
+
+
+E_ON = 8
+
+
+def rank_program(g, core, T, topo):
+    rank = T.rank_of(core)
+    if rank is None:
+        return
+    S = T.sem
+    A, AX, AF = AluOpType, AxisListType, ActivationFunctionType
+    v, s, pe, sy = g.vector, g.scalar, g.tensor, g.sync
+    chips, gate = _plan(T, topo)
+    mine = chips[topo.chip(core)]
+    near = [c for c in mine if c != core]
+    far = [c for c in T.cores if c not in mine]
+    gw = gate[topo.chip(core)]
+    G, sm = T.G, T.sm
+    o = 4 * rank
+    own = G[:, o:o + 4]
+
+    def off_mask(src):
+        m = topo.mask(src, [c for c in T.cores if topo.chip(c) != topo.chip(src)][0])
+        return _low(m, min(8, _bits(m)))
+
+    def on_mask(src, dst):
+        if src == gate[topo.chip(src)]:
+            return _low(off_mask(src) & topo.mask(src, dst), E_ON)
+        return _low(topo.mask(src, dst), E_ON)
+
+    n_on = sum(_bits(on_mask(c, core)) for c in near)
+    n_off = _bits(off_mask(gate[topo.chip(far[0])]))
+
+    sy.dma_start(T.xs[:], T.x[:]).then_inc(S.ldx, 16)
+    s.dma_start(T.dys[:], T.dy[:]).then_inc(S.ldy, 16)
+    v.memset(T.ones[:], 1.0).then_inc(S.ones, 1)
+    v.memset(T.cst[:, 0:1], -1.0 / D).then_inc(S.cst, 1)
+    v.memset(T.cst[:, 1:2], -1.0).then_inc(S.cst, 1)
+    v.memset(G[:, 25:26], 16384.0 * D * EPS).then_inc(S.eps, 1)
+    g.wait_ge(S.ones, 1)
+    g.affine_select(T.ident[:], T.ones[:], [[-1, 128]], A.is_equal, 0.0, 0, 1).then_inc(S.id, 1)
+    s.wait_ge(S.id, 1)
+    s.activation(T.cI[:], T.ident[:], AF.Sqrt, scale=16384.0).then_inc(S.cI, 1)
+
+    pe.wait_ge(S.ldx, 16)
+    pe.wait_ge(S.id, 1)
+    pe.transpose(T.xT[:, 0:128], T.xs[:], T.ident[:]).then_inc(S.xT, 1)
+    pe.wait_ge(S.ldy, 16)
+    pe.wait_ge(S.cst, 2)
+    pe.matmul(T.st[:, 0:1], T.dys[:], T.cst[:, 0:1], True, True).then_inc(S.st, 1)
+    pe.wait_ge(S.prod, 1)
+    pe.matmul(T.st[:, 1:2], T.prod[:], T.cst[:, 1:2], True, True).then_inc(S.st, 1)
+    pe.transpose(T.dyT[:, 0:128], T.dys[:], T.ident[:]).then_inc(S.dyT, 1)
+
+    v.wait_ge(S.ldx, 16)
+    v.wait_ge(S.ldy, 16)
+    v.tensor_tensor(T.prod[:], T.xs[:], T.dys[:], A.mult).then_inc(S.prod, 1)
+    v.wait_ge(S.xT, 1)
+    v.tensor_reduce(G[:, o:o + 1], T.xT[:, 0:128], AX.X, A.add, negate=True).then_inc(S.nS, 1)
+    s.wait_ge(S.nS, 1)
+    s.activation(T.jq[:], T.xT[:, 0:128], AF.Square, bias=G[:, o:o + 1], scale=128.0,
+                 accum_out=G[:, o + 1:o + 2]).then_inc(S.stat, 1)
+    v.wait_ge(S.st, 2)
+    v.tensor_copy(G[:, o + 2:o + 4], T.st[:, 0:2]).then_inc(S.stat, 1)
+
+    def dst(c):
+        rid, pid, _ = topo.addr(c)
+        return DstId(rid=rid, pnc=pid)
+
+    sent = 0
+    g.wait_ge(S.stat, 2)
+    if core != gw:
+        for c in [gw] + [c for c in near if c != gw]:
+            m = on_mask(core, c)
+            rid, pid, _ = topo.addr(c)
+            g.remote_dma(own, own, S.on, S.sent, pid, rid, m)
+            sent += _bits(m)
+    else:
+        m = on_mask(core, near[0])
+        g.remote_dma_fused([RemoteDMATransfer(dst_ids=[dst(c) for c in near], dma_engine_mask=m, remote_sem=S.on,
+                                              srcs=[own], dsts=[own for c in near])], local_sem=S.sent)
+        sent += _bits(m)
+        g.wait_ge(S.on, n_on)
+        lo = 4 * min(T.rank_of(c) for c in mine)
+        blk = G[:, lo:lo + 4 * len(mine)]
+        m = off_mask(core)
+        g.remote_dma_fused([RemoteDMATransfer(dst_ids=[dst(c) for c in far], dma_engine_mask=m, remote_sem=S.off,
+                                              srcs=[blk], dsts=[blk for c in far])], local_sem=S.sent)
+        sent += _bits(m)
+    g.wait_ge(S.sent, sent)
+
+    nb, sQ, sA, SS, sP, nCx = sm[:, 0:1], sm[:, 1:2], sm[:, 2:3], sm[:, 3:4], sm[:, 4:5], sm[:, 5:6]
+    V, iV, r0, k = sm[:, 6:7], sm[:, 7:8], sm[:, 8:9], sm[:, 9:10]
+    for q in (v, s):
+        q.wait_ge(S.stat, 2)
+        q.wait_ge(S.on, n_on)
+        q.wait_ge(S.off, n_off)
+    v.wait_ge(S.eps, 1)
+    v.tensor_reduce(nb, G[:, 0:24:4], AX.X, A.add).then_inc(S.nb, 1)
+    v.tensor_reduce(sQ, G[:, 1:28:4], AX.X, A.add).then_inc(S.sQ, 1)
+    s.activation(T.j0[:, 0:6], G[:, 2:24:4], AF.Identity, accum_out=sA).then_inc(S.sA, 1)
+    s.wait_ge(S.nb, 1)
+    s.activation(T.j1[:, 0:6], G[:, 0:24:4], AF.Square, bias=nb, scale=-6.0, accum_out=SS).then_inc(S.S, 1)
+    s.activation(T.j2[:, 0:6], G[:, 3:24:4], AF.Identity, accum_out=sP).then_inc(S.sP, 1)
+    s.wait_ge(S.sA, 1)
+    s.wait_ge(S.sP, 1)
+    s.activation(nCx, sA, AF.Identity, bias=sP, scale=nb).then_inc(S.nCx, 1)
+    s.wait_ge(S.dyT, 1)
+    s.activation(T.dyc[:], T.dyT[:, 0:128], AF.Identity, bias=sA).then_inc(S.dyc, 1)
+    s.activation(T.dxc[:], T.xT[:, 0:128], AF.Identity, bias=nb, scale=float(D)).then_inc(S.dxc, 1)
+
+    v.wait_ge(S.S, 1)
+    v.wait_ge(S.sQ, 1)
+    v.tensor_scalar(V, SS, 32.0 / 9.0, sQ, A.mult, A.add).then_inc(S.V, 1)
+    v.wait_ge(S.V, 1)
+    v.reciprocal(iV, V).then_inc(S.iV, 1)
+    v.wait_ge(S.iV, 1)
+    v.wait_ge(S.nCx, 1)
+    v.tensor_scalar(k, nCx, iV, 16384.0 / D, A.mult, A.mult).then_inc(S.k, 1)
+    v.wait_ge(S.k, 1)
+    v.wait_ge(S.dxc, 1)
+    v.tensor_scalar(T.z[:, 0:128], T.dxc[:], k, None, A.mult).then_inc(S.z, 1)
+    v.wait_ge(S.z, 1)
+    v.wait_ge(S.dyc, 1)
+    v.tensor_tensor(T.w[:], T.z[:, 0:128], T.dyc[:], A.add).then_inc(S.w, 1)
+
+    s.wait_ge(S.iV, 1)
+    s.activation(r0, iV, AF.Sqrt, scale=float(D)).then_inc(S.r0, 1)
+    s.wait_ge(S.r0, 1)
+    s.wait_ge(S.cI, 1)
+    s.activation(T.diag[:], T.cI[:], AF.Identity, scale=r0).then_inc(S.diag, 1)
+
+    pe.wait_ge(S.w, 1)
+    pe.wait_ge(S.diag, 1)
+    pe.matmul(T.o1[:, 0:64], T.w[0:64, :], T.diag[0:64, 0:64], True, True).then_inc(S.o1, 1)
+    pe.matmul(T.o2[:, 0:64], T.w[64:128, :], T.diag[64:128, 64:128], True, True).then_inc(S.o2, 1)
+    s.wait_ge(S.o1, 1)
+    s.activation(T.dxs[:, 0:64], T.o1[:, 0:64], AF.Copy).then_inc(S.cp, 1)
+    v.wait_ge(S.o2, 1)
+    v.tensor_copy(T.dxs[:, 64:128], T.o2[:, 0:64]).then_inc(S.cp, 1)
+    sy.wait_ge(S.cp, 2)
+    sy.dma_start(T.dx[:], T.dxs[:]).then_inc(S.store, 16)
+    sy.wait_ge(S.store, 16)

@@ -9,17 +9,19 @@ F32 = "float32"
 SCRATCH = {
     "xs": ("sbuf", [128, 128], F32), "dys": ("sbuf", [128, 128], F32), "prod": ("sbuf", [128, 128], F32),
     "ones": ("sbuf", [128, 128], F32), "ident": ("sbuf", [128, 128], F32), "cI": ("sbuf", [128, 128], F32),
+    "sq": ("sbuf", [128, 128], F32), "rt": ("sbuf", [128, 128], F32),
     "cst": ("sbuf", [128, 4], F32), "G": ("sbuf", [128, 28], F32), "sm": ("sbuf", [128, 16], F32),
     "jq": ("sbuf", [128, 128], F32), "j0": ("sbuf", [128, 8], F32), "j1": ("sbuf", [128, 8], F32),
     "j2": ("sbuf", [128, 8], F32),
     "dyc": ("sbuf", [128, 128], F32), "dxc": ("sbuf", [128, 128], F32), "w": ("sbuf", [128, 128], F32),
     "diag": ("sbuf", [128, 128], F32), "dxs": ("sbuf", [128, 128], F32),
-    "xT": ("psum", [128, 512], F32), "dyT": ("psum", [128, 512], F32), "st": ("psum", [128, 512], F32),
+    "xT": ("psum", [128, 512], F32), "dyT": ("psum", [128, 512], F32), "stA": ("psum", [128, 512], F32),
+    "stP": ("psum", [128, 512], F32),
     "z": ("psum", [128, 512], F32), "o1": ("psum", [128, 512], F32), "o2": ("psum", [128, 512], F32),
 }
-SEMAPHORES = ["ldx", "ldy", "ones", "cst", "eps", "id", "cI", "xT", "st", "prod", "dyT", "nS", "stat", "on", "off",
-              "sent", "nb", "sQ", "sA", "S", "sP", "nCx", "dyc", "dxc", "V", "iV", "r0", "diag", "k", "z", "w",
-              "o1", "o2", "cp", "store"]
+SEMAPHORES = ["ldx", "ldy", "ones", "cst", "eps", "id", "cI", "xT", "mA", "mP", "prod", "dyT", "nS", "first", "stat",
+              "on", "off", "sent", "nb", "sQ", "sA", "S", "sP", "nCx", "dyc", "dxc", "V", "iV", "r0", "diag", "k",
+              "z", "w", "o1", "o2", "cp", "store", "sq", "rt"]
 
 
 def _low(mask, k):
@@ -64,7 +66,7 @@ def rank_program(g, core, T, topo):
     gw = gate[topo.chip(core)]
     G, sm = T.G, T.sm
     o = 4 * rank
-    own = G[:, o:o + 4]
+    own, head, tail = G[:, o:o + 4], G[:, o:o + 1], G[:, o + 1:o + 4]
 
     def off_mask(src):
         m = topo.mask(src, [c for c in T.cores if topo.chip(c) != topo.chip(src)][0])
@@ -75,79 +77,87 @@ def rank_program(g, core, T, topo):
             return _low(off_mask(src) & topo.mask(src, dst), E_ON)
         return _low(topo.mask(src, dst), E_ON)
 
-    n_on = sum(_bits(on_mask(c, core)) for c in near)
+    n_on = sum(_bits(on_mask(c, core)) * (2 if gw in (c, core) else 1) for c in near)
     n_off = _bits(off_mask(gate[topo.chip(far[0])]))
 
-    sy.dma_start(T.xs[:], T.x[:]).then_inc(S.ldx, 16)
-    s.dma_start(T.dys[:], T.dy[:]).then_inc(S.ldy, 16)
+    sy.dma_start(T.dys[0:64, :], T.dy[0:64, :]).then_inc(S.ldy, 16)
+    s.dma_start(T.dys[64:128, :], T.dy[64:128, :]).then_inc(S.ldy, 16)
+    sy.dma_start(T.xs[0:64, :], T.x[0:64, :]).then_inc(S.ldx, 16)
+    s.dma_start(T.xs[64:128, :], T.x[64:128, :]).then_inc(S.ldx, 16)
+    v.memset(T.sq[:], 16384.0).then_inc(S.sq, 1)
     v.memset(T.ones[:], 1.0).then_inc(S.ones, 1)
     v.memset(T.cst[:, 0:1], -1.0 / D).then_inc(S.cst, 1)
     v.memset(T.cst[:, 1:2], -1.0).then_inc(S.cst, 1)
-    v.memset(G[:, 25:26], 16384.0 * D * EPS).then_inc(S.eps, 1)
+    v.memset(G[:, 26:27], 16384.0 * D * EPS).then_inc(S.eps, 1)
+    s.wait_ge(S.sq, 1)
+    s.activation(T.rt[:], T.sq[:], AF.Sqrt).then_inc(S.rt, 1)
     g.wait_ge(S.ones, 1)
     g.affine_select(T.ident[:], T.ones[:], [[-1, 128]], A.is_equal, 0.0, 0, 1).then_inc(S.id, 1)
-    s.wait_ge(S.id, 1)
-    s.activation(T.cI[:], T.ident[:], AF.Sqrt, scale=16384.0).then_inc(S.cI, 1)
 
-    pe.wait_ge(S.ldx, 16)
+    pe.wait_ge(S.ldy, 32)
+    pe.wait_ge(S.cst, 2)
+    pe.matmul(T.stA[:, 0:1], T.dys[:], T.cst[:, 0:1], True, True).then_inc(S.mA, 1)
+    pe.wait_ge(S.ldx, 32)
     pe.wait_ge(S.id, 1)
     pe.transpose(T.xT[:, 0:128], T.xs[:], T.ident[:]).then_inc(S.xT, 1)
-    pe.wait_ge(S.ldy, 16)
-    pe.wait_ge(S.cst, 2)
-    pe.matmul(T.st[:, 0:1], T.dys[:], T.cst[:, 0:1], True, True).then_inc(S.st, 1)
     pe.wait_ge(S.prod, 1)
-    pe.matmul(T.st[:, 1:2], T.prod[:], T.cst[:, 1:2], True, True).then_inc(S.st, 1)
+    pe.matmul(T.stP[:, 0:1], T.prod[:], T.cst[:, 1:2], True, True).then_inc(S.mP, 1)
     pe.transpose(T.dyT[:, 0:128], T.dys[:], T.ident[:]).then_inc(S.dyT, 1)
 
-    v.wait_ge(S.ldx, 16)
-    v.wait_ge(S.ldy, 16)
+    v.wait_ge(S.mA, 1)
+    v.tensor_copy(head, T.stA[:, 0:1]).then_inc(S.first, 1)
+    v.wait_ge(S.ldx, 32)
     v.tensor_tensor(T.prod[:], T.xs[:], T.dys[:], A.mult).then_inc(S.prod, 1)
     v.wait_ge(S.xT, 1)
-    v.tensor_reduce(G[:, o:o + 1], T.xT[:, 0:128], AX.X, A.add, negate=True).then_inc(S.nS, 1)
+    v.tensor_reduce(G[:, o + 1:o + 2], T.xT[:, 0:128], AX.X, A.add, negate=True).then_inc(S.nS, 1)
     s.wait_ge(S.nS, 1)
-    s.activation(T.jq[:], T.xT[:, 0:128], AF.Square, bias=G[:, o:o + 1], scale=128.0,
-                 accum_out=G[:, o + 1:o + 2]).then_inc(S.stat, 1)
-    v.wait_ge(S.st, 2)
-    v.tensor_copy(G[:, o + 2:o + 4], T.st[:, 0:2]).then_inc(S.stat, 1)
+    s.activation(T.jq[:], T.xT[:, 0:128], AF.Square, bias=G[:, o + 1:o + 2], scale=128.0,
+                 accum_out=G[:, o + 2:o + 3]).then_inc(S.stat, 1)
+    v.wait_ge(S.mP, 1)
+    v.tensor_copy(G[:, o + 3:o + 4], T.stP[:, 0:1]).then_inc(S.stat, 1)
 
-    def dst(c):
-        rid, pid, _ = topo.addr(c)
-        return DstId(rid=rid, pnc=pid)
+    sent = [0]
 
-    sent = 0
-    g.wait_ge(S.stat, 2)
-    if core != gw:
-        for c in [gw] + [c for c in near if c != gw]:
-            m = on_mask(core, c)
+    def send(piece, dsts, m, sem):
+        ids = []
+        for c in dsts:
             rid, pid, _ = topo.addr(c)
-            g.remote_dma(own, own, S.on, S.sent, pid, rid, m)
-            sent += _bits(m)
+            ids.append(DstId(rid=rid, pnc=pid))
+        g.remote_dma_fused([RemoteDMATransfer(dst_ids=ids, dma_engine_mask=m, remote_sem=sem, srcs=[piece],
+                                              dsts=[piece for c in dsts])], local_sem=S.sent)
+        sent[0] += _bits(m)
+
+    urgent = near if core == gw else [gw]
+    m = on_mask(core, urgent[0])
+    g.wait_ge(S.first, 1)
+    send(head, urgent, m, S.on)
+    g.wait_ge(S.stat, 2)
+    send(tail, urgent, m, S.on)
+    if core != gw:
+        rest = [c for c in near if c != gw]
+        if rest:
+            send(own, rest, on_mask(core, rest[0]), S.on)
     else:
-        m = on_mask(core, near[0])
-        g.remote_dma_fused([RemoteDMATransfer(dst_ids=[dst(c) for c in near], dma_engine_mask=m, remote_sem=S.on,
-                                              srcs=[own], dsts=[own for c in near])], local_sem=S.sent)
-        sent += _bits(m)
         g.wait_ge(S.on, n_on)
         lo = 4 * min(T.rank_of(c) for c in mine)
-        blk = G[:, lo:lo + 4 * len(mine)]
-        m = off_mask(core)
-        g.remote_dma_fused([RemoteDMATransfer(dst_ids=[dst(c) for c in far], dma_engine_mask=m, remote_sem=S.off,
-                                              srcs=[blk], dsts=[blk for c in far])], local_sem=S.sent)
-        sent += _bits(m)
-    g.wait_ge(S.sent, sent)
+        send(G[:, lo:lo + 4 * len(mine)], far, off_mask(core), S.off)
+    g.wait_ge(S.rt, 1)
+    g.affine_select(T.cI[:], T.rt[:], [[-1, 128]], A.is_equal, 0.0, 0, 1).then_inc(S.cI, 1)
+    g.wait_ge(S.sent, sent[0])
 
     nb, sQ, sA, SS, sP, nCx = sm[:, 0:1], sm[:, 1:2], sm[:, 2:3], sm[:, 3:4], sm[:, 4:5], sm[:, 5:6]
     V, iV, r0, k = sm[:, 6:7], sm[:, 7:8], sm[:, 8:9], sm[:, 9:10]
     for q in (v, s):
+        q.wait_ge(S.first, 1)
         q.wait_ge(S.stat, 2)
         q.wait_ge(S.on, n_on)
         q.wait_ge(S.off, n_off)
     v.wait_ge(S.eps, 1)
-    v.tensor_reduce(nb, G[:, 0:24:4], AX.X, A.add).then_inc(S.nb, 1)
-    v.tensor_reduce(sQ, G[:, 1:28:4], AX.X, A.add).then_inc(S.sQ, 1)
-    s.activation(T.j0[:, 0:6], G[:, 2:24:4], AF.Identity, accum_out=sA).then_inc(S.sA, 1)
+    v.tensor_reduce(nb, G[:, 1:24:4], AX.X, A.add).then_inc(S.nb, 1)
+    v.tensor_reduce(sQ, G[:, 2:28:4], AX.X, A.add).then_inc(S.sQ, 1)
+    s.activation(T.j0[:, 0:6], G[:, 0:24:4], AF.Identity, accum_out=sA).then_inc(S.sA, 1)
     s.wait_ge(S.nb, 1)
-    s.activation(T.j1[:, 0:6], G[:, 0:24:4], AF.Square, bias=nb, scale=-6.0, accum_out=SS).then_inc(S.S, 1)
+    s.activation(T.j1[:, 0:6], G[:, 1:24:4], AF.Square, bias=nb, scale=-6.0, accum_out=SS).then_inc(S.S, 1)
     s.activation(T.j2[:, 0:6], G[:, 3:24:4], AF.Identity, accum_out=sP).then_inc(S.sP, 1)
     s.wait_ge(S.sA, 1)
     s.wait_ge(S.sP, 1)

@@ -5,23 +5,26 @@ N = 6
 D = 128 * N
 EPS = 0.01
 F32 = "float32"
+HB = 16
+HM = (HB + 128) // 2
+W = 8
 
 SCRATCH = {
     "xs": ("sbuf", [128, 128], F32), "dys": ("sbuf", [128, 128], F32), "prod": ("sbuf", [128, 128], F32),
     "ones": ("sbuf", [128, 128], F32), "ident": ("sbuf", [128, 128], F32), "cI": ("sbuf", [128, 128], F32),
     "sq": ("sbuf", [128, 128], F32), "rt": ("sbuf", [128, 128], F32),
-    "cst": ("sbuf", [128, 4], F32), "G": ("sbuf", [128, 28], F32), "sm": ("sbuf", [128, 16], F32),
-    "jq": ("sbuf", [128, 128], F32), "j0": ("sbuf", [128, 8], F32), "j1": ("sbuf", [128, 8], F32),
-    "j2": ("sbuf", [128, 8], F32),
+    "cst": ("sbuf", [128, 4], F32), "G": ("sbuf", [128, 56], F32), "sm": ("sbuf", [128, 16], F32),
+    "jq": ("sbuf", [128, 128], F32), "jn": ("sbuf", [128, 128], F32), "j0": ("sbuf", [128, 16], F32),
+    "j1": ("sbuf", [128, 8], F32),
     "dyc": ("sbuf", [128, 128], F32), "dxc": ("sbuf", [128, 128], F32), "w": ("sbuf", [128, 128], F32),
-    "diag": ("sbuf", [128, 128], F32), "dxs": ("sbuf", [128, 128], F32),
-    "xT": ("psum", [128, 512], F32), "dyT": ("psum", [128, 512], F32), "stA": ("psum", [128, 512], F32),
-    "stP": ("psum", [128, 512], F32),
+    "diag": ("sbuf", [128, 128], F32), "dxa": ("sbuf", [128, 64], F32), "dxb": ("sbuf", [128, 64], F32),
+    "xT": ("psum", [128, 512], F32), "dyT": ("psum", [128, 512], F32), "stH": ("psum", [128, 512], F32),
+    "stA": ("psum", [128, 512], F32), "stP": ("psum", [128, 512], F32),
     "z": ("psum", [128, 512], F32), "o1": ("psum", [128, 512], F32), "o2": ("psum", [128, 512], F32),
 }
-SEMAPHORES = ["ldx", "ldy", "ones", "cst", "eps", "id", "cI", "xT", "mA", "mP", "prod", "dyT", "nS", "first", "stat",
-              "on", "off", "sent", "nb", "sQ", "sA", "S", "sP", "nCx", "dyc", "dxc", "V", "iV", "r0", "diag", "k",
-              "z", "w", "o1", "o2", "cp", "store", "sq", "rt"]
+SEMAPHORES = ["ldh", "ldx", "ldy", "ones", "c0", "cz", "cst", "eps", "id", "cI", "xT", "mH", "mA", "mP", "prod", "dyT",
+              "nS", "first", "stat", "on", "off", "sent", "nb", "sQ", "sA", "S", "sP", "nCx", "nCk", "dyc", "dxc", "V",
+              "iV", "r0", "diag", "z", "w", "o1", "o2", "cpa", "cpb", "store", "sq", "rt"]
 
 
 def _low(mask, k):
@@ -65,8 +68,10 @@ def rank_program(g, core, T, topo):
     far = [c for c in T.cores if c not in mine]
     gw = gate[topo.chip(core)]
     G, sm = T.G, T.sm
-    o = 4 * rank
-    own, head, tail = G[:, o:o + 4], G[:, o:o + 1], G[:, o + 1:o + 4]
+    o = W * rank
+    own, head, tail = G[:, o:o + 8], G[:, o:o + 4], G[:, o + 4:o + 8]
+    cH, cN, cQ, cP, cA = (G[:, o + i:o + i + 1] for i in (3, 4, 5, 6, 7))
+    NW = N * W
 
     def off_mask(src):
         m = topo.mask(src, [c for c in T.cores if topo.chip(c) != topo.chip(src)][0])
@@ -80,41 +85,53 @@ def rank_program(g, core, T, topo):
     n_on = sum(_bits(on_mask(c, core)) * (2 if gw in (c, core) else 1) for c in near)
     n_off = _bits(off_mask(gate[topo.chip(far[0])]))
 
-    sy.dma_start(T.dys[0:64, :], T.dy[0:64, :]).then_inc(S.ldy, 16)
-    s.dma_start(T.dys[64:128, :], T.dy[64:128, :]).then_inc(S.ldy, 16)
-    sy.dma_start(T.xs[0:64, :], T.x[0:64, :]).then_inc(S.ldx, 16)
+    sy.dma_start(T.dys[0:HB, :], T.dy[0:HB, :]).then_inc(S.ldh, 16)
     s.dma_start(T.xs[64:128, :], T.x[64:128, :]).then_inc(S.ldx, 16)
-    v.memset(T.sq[:], 16384.0).then_inc(S.sq, 1)
+    sy.dma_start(T.xs[0:64, :], T.x[0:64, :]).then_inc(S.ldx, 16)
+    s.dma_start(T.dys[HM:128, :], T.dy[HM:128, :]).then_inc(S.ldy, 16)
+    sy.dma_start(T.dys[HB:HM, :], T.dy[HB:HM, :]).then_inc(S.ldy, 16)
+    v.memset(T.cst[:, 0:1], -1.0 / D).then_inc(S.c0, 1)
+    v.memset(G[:, o:o + 3], 0.0).then_inc(S.first, 1)
     v.memset(T.ones[:], 1.0).then_inc(S.ones, 1)
-    v.memset(T.cst[:, 0:1], -1.0 / D).then_inc(S.cst, 1)
-    v.memset(T.cst[:, 1:2], -1.0).then_inc(S.cst, 1)
-    v.memset(G[:, 26:27], 16384.0 * D * EPS).then_inc(S.eps, 1)
-    s.wait_ge(S.sq, 1)
-    s.activation(T.rt[:], T.sq[:], AF.Sqrt).then_inc(S.rt, 1)
+    v.memset(T.cst[:, 1:2], -1.0 / D).then_inc(S.cz, 1)
+    v.memset(T.cst[:, 2:3], -1.0).then_inc(S.cst, 1)
+    v.wait_ge(S.cz, 1)
+    v.memset(T.cst[0:HB, 1:2], 0.0).then_inc(S.cst, 1)
+    v.memset(G[:, NW + 5:NW + 6], 16384.0 * D * EPS).then_inc(S.eps, 1)
+    v.memset(T.sq[:], 16384.0).then_inc(S.sq, 1)
     g.wait_ge(S.ones, 1)
     g.affine_select(T.ident[:], T.ones[:], [[-1, 128]], A.is_equal, 0.0, 0, 1).then_inc(S.id, 1)
 
-    pe.wait_ge(S.ldy, 32)
-    pe.wait_ge(S.cst, 2)
-    pe.matmul(T.stA[:, 0:1], T.dys[:], T.cst[:, 0:1], True, True).then_inc(S.mA, 1)
+    pe.wait_ge(S.ldh, 16)
+    pe.wait_ge(S.c0, 1)
+    pe.matmul(T.stH[:, 0:1], T.dys[0:HB, :], T.cst[0:HB, 0:1], True, True).then_inc(S.mH, 1)
     pe.wait_ge(S.ldx, 32)
     pe.wait_ge(S.id, 1)
     pe.transpose(T.xT[:, 0:128], T.xs[:], T.ident[:]).then_inc(S.xT, 1)
+    pe.wait_ge(S.ldy, 32)
+    pe.wait_ge(S.cst, 2)
+    pe.matmul(T.stA[:, 0:1], T.dys[:], T.cst[:, 1:2], True, True).then_inc(S.mA, 1)
     pe.wait_ge(S.prod, 1)
-    pe.matmul(T.stP[:, 0:1], T.prod[:], T.cst[:, 1:2], True, True).then_inc(S.mP, 1)
+    pe.matmul(T.stP[:, 0:1], T.prod[:], T.cst[:, 2:3], True, True).then_inc(S.mP, 1)
     pe.transpose(T.dyT[:, 0:128], T.dys[:], T.ident[:]).then_inc(S.dyT, 1)
 
-    v.wait_ge(S.mA, 1)
-    v.tensor_copy(head, T.stA[:, 0:1]).then_inc(S.first, 1)
+    v.wait_ge(S.mH, 1)
+    v.tensor_copy(cH, T.stH[:, 0:1]).then_inc(S.first, 1)
+    v.wait_ge(S.ldh, 16)
     v.wait_ge(S.ldx, 32)
+    v.wait_ge(S.ldy, 32)
     v.tensor_tensor(T.prod[:], T.xs[:], T.dys[:], A.mult).then_inc(S.prod, 1)
-    v.wait_ge(S.xT, 1)
-    v.tensor_reduce(G[:, o + 1:o + 2], T.xT[:, 0:128], AX.X, A.add, negate=True).then_inc(S.nS, 1)
-    s.wait_ge(S.nS, 1)
-    s.activation(T.jq[:], T.xT[:, 0:128], AF.Square, bias=G[:, o + 1:o + 2], scale=128.0,
-                 accum_out=G[:, o + 2:o + 3]).then_inc(S.stat, 1)
+    v.wait_ge(S.mA, 1)
+    v.tensor_copy(cA, T.stA[:, 0:1]).then_inc(S.stat, 1)
     v.wait_ge(S.mP, 1)
-    v.tensor_copy(G[:, o + 3:o + 4], T.stP[:, 0:1]).then_inc(S.stat, 1)
+    v.tensor_copy(cP, T.stP[:, 0:1]).then_inc(S.stat, 1)
+
+    s.wait_ge(S.xT, 1)
+    s.activation(T.jn[:], T.xT[:, 0:128], AF.Identity, scale=-1.0, accum_out=cN).then_inc(S.nS, 1)
+    s.wait_ge(S.nS, 1)
+    s.activation(T.jq[:], T.xT[:, 0:128], AF.Square, bias=cN, scale=128.0, accum_out=cQ).then_inc(S.stat, 1)
+    s.wait_ge(S.sq, 1)
+    s.activation(T.rt[:], T.sq[:], AF.Sqrt).then_inc(S.rt, 1)
 
     sent = [0]
 
@@ -129,9 +146,9 @@ def rank_program(g, core, T, topo):
 
     urgent = near if core == gw else [gw]
     m = on_mask(core, urgent[0])
-    g.wait_ge(S.first, 1)
+    g.wait_ge(S.first, 2)
     send(head, urgent, m, S.on)
-    g.wait_ge(S.stat, 2)
+    g.wait_ge(S.stat, 3)
     send(tail, urgent, m, S.on)
     if core != gw:
         rest = [c for c in near if c != gw]
@@ -139,32 +156,34 @@ def rank_program(g, core, T, topo):
             send(own, rest, on_mask(core, rest[0]), S.on)
     else:
         g.wait_ge(S.on, n_on)
-        lo = 4 * min(T.rank_of(c) for c in mine)
-        send(G[:, lo:lo + 4 * len(mine)], far, off_mask(core), S.off)
+        lo = W * min(T.rank_of(c) for c in mine)
+        send(G[:, lo + 3:lo + W * len(mine)], far, off_mask(core), S.off)
     g.wait_ge(S.rt, 1)
     g.affine_select(T.cI[:], T.rt[:], [[-1, 128]], A.is_equal, 0.0, 0, 1).then_inc(S.cI, 1)
     g.wait_ge(S.sent, sent[0])
 
     nb, sQ, sA, SS, sP, nCx = sm[:, 0:1], sm[:, 1:2], sm[:, 2:3], sm[:, 3:4], sm[:, 4:5], sm[:, 5:6]
-    V, iV, r0, k = sm[:, 6:7], sm[:, 7:8], sm[:, 8:9], sm[:, 9:10]
+    V, iV, r0, nCk = sm[:, 6:7], sm[:, 7:8], sm[:, 8:9], sm[:, 9:10]
     for q in (v, s):
-        q.wait_ge(S.first, 1)
-        q.wait_ge(S.stat, 2)
+        q.wait_ge(S.first, 2)
+        q.wait_ge(S.stat, 3)
         q.wait_ge(S.on, n_on)
         q.wait_ge(S.off, n_off)
     v.wait_ge(S.eps, 1)
-    v.tensor_reduce(nb, G[:, 1:24:4], AX.X, A.add).then_inc(S.nb, 1)
-    v.tensor_reduce(sQ, G[:, 2:28:4], AX.X, A.add).then_inc(S.sQ, 1)
-    s.activation(T.j0[:, 0:6], G[:, 0:24:4], AF.Identity, accum_out=sA).then_inc(S.sA, 1)
+    v.tensor_reduce(nb, G[:, 4:NW:W], AX.X, A.add).then_inc(S.nb, 1)
+    v.tensor_reduce(sQ, G[:, 5:NW + W:W], AX.X, A.add).then_inc(S.sQ, 1)
+    v.tensor_reduce(sP, G[:, 6:NW:W], AX.X, A.add).then_inc(S.sP, 1)
+    s.activation(T.j0[:, 0:12], G[:, 3:NW:4], AF.Identity, accum_out=sA).then_inc(S.sA, 1)
     s.wait_ge(S.nb, 1)
-    s.activation(T.j1[:, 0:6], G[:, 1:24:4], AF.Square, bias=nb, scale=-6.0, accum_out=SS).then_inc(S.S, 1)
-    s.activation(T.j2[:, 0:6], G[:, 3:24:4], AF.Identity, accum_out=sP).then_inc(S.sP, 1)
+    s.activation(T.j1[:, 0:6], G[:, 4:NW:W], AF.Square, bias=nb, scale=-6.0, accum_out=SS).then_inc(S.S, 1)
     s.wait_ge(S.sA, 1)
     s.wait_ge(S.sP, 1)
     s.activation(nCx, sA, AF.Identity, bias=sP, scale=nb).then_inc(S.nCx, 1)
+    s.wait_ge(S.nCx, 1)
+    s.activation(nCk, nCx, AF.Copy, scale=16384.0 / D).then_inc(S.nCk, 1)
+    s.activation(T.dxc[:], T.xT[:, 0:128], AF.Identity, bias=nb, scale=float(D)).then_inc(S.dxc, 1)
     s.wait_ge(S.dyT, 1)
     s.activation(T.dyc[:], T.dyT[:, 0:128], AF.Identity, bias=sA).then_inc(S.dyc, 1)
-    s.activation(T.dxc[:], T.xT[:, 0:128], AF.Identity, bias=nb, scale=float(D)).then_inc(S.dxc, 1)
 
     v.wait_ge(S.S, 1)
     v.wait_ge(S.sQ, 1)
@@ -172,11 +191,9 @@ def rank_program(g, core, T, topo):
     v.wait_ge(S.V, 1)
     v.reciprocal(iV, V).then_inc(S.iV, 1)
     v.wait_ge(S.iV, 1)
-    v.wait_ge(S.nCx, 1)
-    v.tensor_scalar(k, nCx, iV, 16384.0 / D, A.mult, A.mult).then_inc(S.k, 1)
-    v.wait_ge(S.k, 1)
+    v.wait_ge(S.nCk, 1)
     v.wait_ge(S.dxc, 1)
-    v.tensor_scalar(T.z[:, 0:128], T.dxc[:], k, None, A.mult).then_inc(S.z, 1)
+    v.tensor_scalar(T.z[:, 0:128], T.dxc[:], iV, nCk, A.mult, A.mult).then_inc(S.z, 1)
     v.wait_ge(S.z, 1)
     v.wait_ge(S.dyc, 1)
     v.tensor_tensor(T.w[:], T.z[:, 0:128], T.dyc[:], A.add).then_inc(S.w, 1)
@@ -192,9 +209,11 @@ def rank_program(g, core, T, topo):
     pe.matmul(T.o1[:, 0:64], T.w[0:64, :], T.diag[0:64, 0:64], True, True).then_inc(S.o1, 1)
     pe.matmul(T.o2[:, 0:64], T.w[64:128, :], T.diag[64:128, 64:128], True, True).then_inc(S.o2, 1)
     s.wait_ge(S.o1, 1)
-    s.activation(T.dxs[:, 0:64], T.o1[:, 0:64], AF.Copy).then_inc(S.cp, 1)
+    s.activation(T.dxa[:], T.o1[:, 0:64], AF.Copy).then_inc(S.cpa, 1)
     v.wait_ge(S.o2, 1)
-    v.tensor_copy(T.dxs[:, 64:128], T.o2[:, 0:64]).then_inc(S.cp, 1)
-    sy.wait_ge(S.cp, 2)
-    sy.dma_start(T.dx[:], T.dxs[:]).then_inc(S.store, 16)
-    sy.wait_ge(S.store, 16)
+    v.tensor_copy(T.dxb[:], T.o2[:, 0:64]).then_inc(S.cpb, 1)
+    sy.wait_ge(S.cpa, 1)
+    sy.dma_start(T.dx[:, 0:64], T.dxa[:]).then_inc(S.store, 16)
+    sy.wait_ge(S.cpb, 1)
+    sy.dma_start(T.dx[:, 64:128], T.dxb[:]).then_inc(S.store, 16)
+    sy.wait_ge(S.store, 32)

from concourse.bass import DstId, RemoteDMATransfer
from concourse.mybir import AluOpType, AxisListType, ActivationFunctionType

N = 6
D = 128 * N
EPS = 0.01
F32 = "float32"
HB = 16
HM = (HB + 128) // 2
W = 8

SCRATCH = {
    "xs": ("sbuf", [128, 128], F32), "dys": ("sbuf", [128, 128], F32), "prod": ("sbuf", [128, 128], F32),
    "ones": ("sbuf", [128, 128], F32), "ident": ("sbuf", [128, 128], F32), "cI": ("sbuf", [128, 128], F32),
    "sq": ("sbuf", [128, 128], F32), "rt": ("sbuf", [128, 128], F32),
    "cst": ("sbuf", [128, 4], F32), "G": ("sbuf", [128, 56], F32), "sm": ("sbuf", [128, 16], F32),
    "jq": ("sbuf", [128, 128], F32), "jn": ("sbuf", [128, 128], F32), "j0": ("sbuf", [128, 16], F32),
    "j1": ("sbuf", [128, 8], F32),
    "dyc": ("sbuf", [128, 128], F32), "dxc": ("sbuf", [128, 128], F32), "w": ("sbuf", [128, 128], F32),
    "diag": ("sbuf", [128, 128], F32), "dxa": ("sbuf", [128, 64], F32), "dxb": ("sbuf", [128, 64], F32),
    "xT": ("psum", [128, 512], F32), "dyT": ("psum", [128, 512], F32), "stH": ("psum", [128, 512], F32),
    "stA": ("psum", [128, 512], F32), "stP": ("psum", [128, 512], F32),
    "z": ("psum", [128, 512], F32), "o1": ("psum", [128, 512], F32), "o2": ("psum", [128, 512], F32),
}
SEMAPHORES = ["ldh", "ldx", "ldy", "ones", "c0", "cz", "cst", "eps", "id", "cI", "xT", "mH", "mA", "mP", "prod", "dyT",
              "nS", "first", "stat", "on", "off", "sent", "nb", "sQ", "sA", "S", "sP", "nCx", "nCk", "dyc", "dxc", "V",
              "iV", "r0", "diag", "z", "w", "o1", "o2", "cpa", "cpb", "store", "sq", "rt"]


def _low(mask, k):
    out, b = 0, 1
    while k and b <= mask:
        if mask & b:
            out |= b
            k -= 1
        b <<= 1
    return out


def _bits(mask):
    return bin(mask).count("1")


def _plan(T, topo):
    chips = {}
    for c in T.cores:
        chips.setdefault(topo.chip(c), []).append(c)
    gate = {}
    for ch, mem in chips.items():
        far = [c for c in T.cores if topo.chip(c) != ch]
        gate[ch] = [m for m in mem if all(topo.may_write(m, o) for o in far)][0]
    return chips, gate


E_ON = 8


def rank_program(g, core, T, topo):
    rank = T.rank_of(core)
    if rank is None:
        return
    S = T.sem
    A, AX, AF = AluOpType, AxisListType, ActivationFunctionType
    v, s, pe, sy = g.vector, g.scalar, g.tensor, g.sync
    chips, gate = _plan(T, topo)
    mine = chips[topo.chip(core)]
    near = [c for c in mine if c != core]
    far = [c for c in T.cores if c not in mine]
    gw = gate[topo.chip(core)]
    G, sm = T.G, T.sm
    o = W * rank
    own, head, tail = G[:, o:o + 8], G[:, o:o + 4], G[:, o + 4:o + 8]
    cH, cN, cQ, cP, cA = (G[:, o + i:o + i + 1] for i in (3, 4, 5, 6, 7))
    NW = N * W

    def off_mask(src):
        m = topo.mask(src, [c for c in T.cores if topo.chip(c) != topo.chip(src)][0])
        return _low(m, min(8, _bits(m)))

    def on_mask(src, dst):
        if src == gate[topo.chip(src)]:
            return _low(off_mask(src) & topo.mask(src, dst), E_ON)
        return _low(topo.mask(src, dst), E_ON)

    n_on = sum(_bits(on_mask(c, core)) * (2 if gw in (c, core) else 1) for c in near)
    n_off = _bits(off_mask(gate[topo.chip(far[0])]))

    sy.dma_start(T.dys[0:HB, :], T.dy[0:HB, :]).then_inc(S.ldh, 16)
    s.dma_start(T.xs[64:128, :], T.x[64:128, :]).then_inc(S.ldx, 16)
    sy.dma_start(T.xs[0:64, :], T.x[0:64, :]).then_inc(S.ldx, 16)
    s.dma_start(T.dys[HM:128, :], T.dy[HM:128, :]).then_inc(S.ldy, 16)
    sy.dma_start(T.dys[HB:HM, :], T.dy[HB:HM, :]).then_inc(S.ldy, 16)
    v.memset(T.cst[:, 0:1], -1.0 / D).then_inc(S.c0, 1)
    v.memset(G[:, o:o + 3], 0.0).then_inc(S.first, 1)
    v.memset(T.ones[:], 1.0).then_inc(S.ones, 1)
    v.memset(T.cst[:, 1:2], -1.0 / D).then_inc(S.cz, 1)
    v.memset(T.cst[:, 2:3], -1.0).then_inc(S.cst, 1)
    v.wait_ge(S.cz, 1)
    v.memset(T.cst[0:HB, 1:2], 0.0).then_inc(S.cst, 1)
    v.memset(G[:, NW + 5:NW + 6], 16384.0 * D * EPS).then_inc(S.eps, 1)
    v.memset(T.sq[:], 16384.0).then_inc(S.sq, 1)
    g.wait_ge(S.ones, 1)
    g.affine_select(T.ident[:], T.ones[:], [[-1, 128]], A.is_equal, 0.0, 0, 1).then_inc(S.id, 1)

    pe.wait_ge(S.ldh, 16)
    pe.wait_ge(S.c0, 1)
    pe.matmul(T.stH[:, 0:1], T.dys[0:HB, :], T.cst[0:HB, 0:1], True, True).then_inc(S.mH, 1)
    pe.wait_ge(S.ldx, 32)
    pe.wait_ge(S.id, 1)
    pe.transpose(T.xT[:, 0:128], T.xs[:], T.ident[:]).then_inc(S.xT, 1)
    pe.wait_ge(S.ldy, 32)
    pe.wait_ge(S.cst, 2)
    pe.matmul(T.stA[:, 0:1], T.dys[:], T.cst[:, 1:2], True, True).then_inc(S.mA, 1)
    pe.wait_ge(S.prod, 1)
    pe.matmul(T.stP[:, 0:1], T.prod[:], T.cst[:, 2:3], True, True).then_inc(S.mP, 1)
    pe.transpose(T.dyT[:, 0:128], T.dys[:], T.ident[:]).then_inc(S.dyT, 1)

    v.wait_ge(S.mH, 1)
    v.tensor_copy(cH, T.stH[:, 0:1]).then_inc(S.first, 1)
    v.wait_ge(S.ldh, 16)
    v.wait_ge(S.ldx, 32)
    v.wait_ge(S.ldy, 32)
    v.tensor_tensor(T.prod[:], T.xs[:], T.dys[:], A.mult).then_inc(S.prod, 1)
    v.wait_ge(S.mA, 1)
    v.tensor_copy(cA, T.stA[:, 0:1]).then_inc(S.stat, 1)
    v.wait_ge(S.mP, 1)
    v.tensor_copy(cP, T.stP[:, 0:1]).then_inc(S.stat, 1)

    s.wait_ge(S.xT, 1)
    s.activation(T.jn[:], T.xT[:, 0:128], AF.Identity, scale=-1.0, accum_out=cN).then_inc(S.nS, 1)
    s.wait_ge(S.nS, 1)
    s.activation(T.jq[:], T.xT[:, 0:128], AF.Square, bias=cN, scale=128.0, accum_out=cQ).then_inc(S.stat, 1)
    s.wait_ge(S.sq, 1)
    s.activation(T.rt[:], T.sq[:], AF.Sqrt).then_inc(S.rt, 1)

    sent = [0]

    def send(piece, dsts, m, sem):
        ids = []
        for c in dsts:
            rid, pid, _ = topo.addr(c)
            ids.append(DstId(rid=rid, pnc=pid))
        g.remote_dma_fused([RemoteDMATransfer(dst_ids=ids, dma_engine_mask=m, remote_sem=sem, srcs=[piece],
                                              dsts=[piece for c in dsts])], local_sem=S.sent)
        sent[0] += _bits(m)

    urgent = near if core == gw else [gw]
    m = on_mask(core, urgent[0])
    g.wait_ge(S.first, 2)
    send(head, urgent, m, S.on)
    g.wait_ge(S.stat, 3)
    send(tail, urgent, m, S.on)
    if core != gw:
        rest = [c for c in near if c != gw]
        if rest:
            send(own, rest, on_mask(core, rest[0]), S.on)
    else:
        g.wait_ge(S.on, n_on)
        lo = W * min(T.rank_of(c) for c in mine)
        send(G[:, lo + 3:lo + W * len(mine)], far, off_mask(core), S.off)
    g.wait_ge(S.rt, 1)
    g.affine_select(T.cI[:], T.rt[:], [[-1, 128]], A.is_equal, 0.0, 0, 1).then_inc(S.cI, 1)
    g.wait_ge(S.sent, sent[0])

    nb, sQ, sA, SS, sP, nCx = sm[:, 0:1], sm[:, 1:2], sm[:, 2:3], sm[:, 3:4], sm[:, 4:5], sm[:, 5:6]
    V, iV, r0, nCk = sm[:, 6:7], sm[:, 7:8], sm[:, 8:9], sm[:, 9:10]
    for q in (v, s):
        q.wait_ge(S.first, 2)
        q.wait_ge(S.stat, 3)
        q.wait_ge(S.on, n_on)
        q.wait_ge(S.off, n_off)
    v.wait_ge(S.eps, 1)
    v.tensor_reduce(nb, G[:, 4:NW:W], AX.X, A.add).then_inc(S.nb, 1)
    v.tensor_reduce(sQ, G[:, 5:NW + W:W], AX.X, A.add).then_inc(S.sQ, 1)
    v.tensor_reduce(sP, G[:, 6:NW:W], AX.X, A.add).then_inc(S.sP, 1)
    s.activation(T.j0[:, 0:12], G[:, 3:NW:4], AF.Identity, accum_out=sA).then_inc(S.sA, 1)
    s.wait_ge(S.nb, 1)
    s.activation(T.j1[:, 0:6], G[:, 4:NW:W], AF.Square, bias=nb, scale=-6.0, accum_out=SS).then_inc(S.S, 1)
    s.wait_ge(S.sA, 1)
    s.wait_ge(S.sP, 1)
    s.activation(nCx, sA, AF.Identity, bias=sP, scale=nb).then_inc(S.nCx, 1)
    s.wait_ge(S.nCx, 1)
    s.activation(nCk, nCx, AF.Copy, scale=16384.0 / D).then_inc(S.nCk, 1)
    s.activation(T.dxc[:], T.xT[:, 0:128], AF.Identity, bias=nb, scale=float(D)).then_inc(S.dxc, 1)
    s.wait_ge(S.dyT, 1)
    s.activation(T.dyc[:], T.dyT[:, 0:128], AF.Identity, bias=sA).then_inc(S.dyc, 1)

    v.wait_ge(S.S, 1)
    v.wait_ge(S.sQ, 1)
    v.tensor_scalar(V, SS, 32.0 / 9.0, sQ, A.mult, A.add).then_inc(S.V, 1)
    v.wait_ge(S.V, 1)
    v.reciprocal(iV, V).then_inc(S.iV, 1)
    v.wait_ge(S.iV, 1)
    v.wait_ge(S.nCk, 1)
    v.wait_ge(S.dxc, 1)
    v.tensor_scalar(T.z[:, 0:128], T.dxc[:], iV, nCk, A.mult, A.mult).then_inc(S.z, 1)
    v.wait_ge(S.z, 1)
    v.wait_ge(S.dyc, 1)
    v.tensor_tensor(T.w[:], T.z[:, 0:128], T.dyc[:], A.add).then_inc(S.w, 1)

    s.wait_ge(S.iV, 1)
    s.activation(r0, iV, AF.Sqrt, scale=float(D)).then_inc(S.r0, 1)
    s.wait_ge(S.r0, 1)
    s.wait_ge(S.cI, 1)
    s.activation(T.diag[:], T.cI[:], AF.Identity, scale=r0).then_inc(S.diag, 1)

    pe.wait_ge(S.w, 1)
    pe.wait_ge(S.diag, 1)
    pe.matmul(T.o1[:, 0:64], T.w[0:64, :], T.diag[0:64, 0:64], True, True).then_inc(S.o1, 1)
    pe.matmul(T.o2[:, 0:64], T.w[64:128, :], T.diag[64:128, 64:128], True, True).then_inc(S.o2, 1)
    s.wait_ge(S.o1, 1)
    s.activation(T.dxa[:], T.o1[:, 0:64], AF.Copy).then_inc(S.cpa, 1)
    v.wait_ge(S.o2, 1)
    v.tensor_copy(T.dxb[:], T.o2[:, 0:64]).then_inc(S.cpb, 1)
    sy.wait_ge(S.cpa, 1)
    sy.dma_start(T.dx[:, 0:64], T.dxa[:]).then_inc(S.store, 16)
    sy.wait_ge(S.cpb, 1)
    sy.dma_start(T.dx[:, 64:128], T.dxb[:]).then_inc(S.store, 16)
    sy.wait_ge(S.store, 32)
